import numpy as np
import ml_dtypes


def mxq(x, axis, fmt="e4m3"):
    dtype, down = {"e4m3": (ml_dtypes.float8_e4m3fn, 7), "e5m2": (ml_dtypes.float8_e5m2, 14)}[fmt]
    v = np.moveaxis(np.asarray(x, np.float32).astype(ml_dtypes.bfloat16).astype(np.float64), axis, -1)
    blocks = v.reshape(v.shape[:-1] + (-1, 32))
    amax = np.abs(blocks).max(-1, keepdims=True)
    byte = np.maximum(np.where(amax > 0, np.frexp(amax)[1] - 1 + 127, 0) - down, 1)
    scale = np.exp2(byte - 127.0)
    codes = (blocks / scale).astype(np.float32).astype(dtype).astype(np.float64)
    return np.moveaxis((codes * scale).reshape(v.shape), -1, axis)


WIDE = False


def mx_kscale(k):
    if not WIDE:
        return np.ones(k)
    levels = np.array([30, -30])
    if k % 512:
        return np.exp2(np.random.permutation(np.resize(levels, k // 32))).repeat(32)
    a = np.empty((k // 512, 16))
    for p in range(k // 512):
        a[p, :8] = np.random.permutation(np.resize(levels, 8))
        for g in range(8):
            far = levels[np.abs(levels - a[p, g]) >= 10]
            a[p, g + 8] = far[np.random.randint(len(far))]
    return np.exp2(a.ravel()).repeat(32)


def f64(x):
    return np.asarray(x).astype(np.float64)


def striped(idx):
    return np.tile(np.asarray(idx).reshape(-1, 16).T, (8, 1)).astype(np.uint16)


def unstriped(offs):
    return offs[:16].T.reshape(-1).astype(np.int64)


def striped8(idx):
    return np.asarray(idx).reshape(8, -1, 16).transpose(0, 2, 1).reshape(128, -1).astype(np.uint16)


def unstriped8(offs):
    return offs.reshape(8, 16, -1).transpose(0, 2, 1).reshape(8, -1).astype(np.int64)


def pick8(x, idx, run):
    r = np.arange(len(x))
    return x[r[:, None], idx[r % (8 * run) // run]]


E2M1 = np.array([0.0, 0.5, 1.0, 1.5, 2.0, 3.0, 4.0, 6.0, -0.0, -0.5, -1.0, -1.5, -2.0, -3.0, -4.0, -6.0])


def pack_weight(w, fmt):
    k, n = w.shape
    w = f64(np.asarray(w, np.float32).astype(ml_dtypes.bfloat16)).reshape(k // 32, 32, n)
    amax = np.abs(w).max(1)
    if fmt in ("e4m3", "e5m2"):
        byte = np.frexp(amax)[1] - 1 + 127 - (7 if fmt == "e4m3" else 14)
    else:
        mant, ex = np.frexp(amax / 6.0)
        byte = np.where(mant > 0.5, ex, ex - 1) + 127
    byte = np.clip(np.where(amax > 0, byte, 1), 1, 254)
    scaled = (w * np.exp2(127.0 - byte)[:, None, :]).reshape(k, n).astype(np.float32)
    by_word = np.ascontiguousarray(scaled.reshape(k // 512, 128, 4, n).transpose(0, 1, 3, 2))
    if fmt in ("e4m3", "e5m2"):
        words = by_word.astype(ml_dtypes.float8_e4m3fn if fmt == "e4m3" else ml_dtypes.float8_e5m2).view(np.uint8)
    else:
        c = by_word.astype(ml_dtypes.float4_e2m1fn).view(np.uint8) & 0xF
        words = (c[..., 0::2] | (c[..., 1::2] << 4)).reshape(k // 512, 128, 2 * n)
    return np.ascontiguousarray(words), np.ascontiguousarray(byte.astype(np.uint8).reshape(k // 512, 16, n))


def unpack_weight(words, scales, fmt):
    g, _, n = scales.shape
    words = np.ascontiguousarray(words).reshape(g, 128, n, -1)
    if fmt in ("e4m3", "e5m2"):
        vals = words.view(ml_dtypes.float8_e4m3fn if fmt == "e4m3" else ml_dtypes.float8_e5m2).astype(np.float64)
    else:
        nib = np.empty((g, 128, n, 4), np.uint8)
        nib[..., 0::2] = words & 0xF
        nib[..., 1::2] = words >> 4
        vals = E2M1[nib]
    vals = vals * np.repeat(np.exp2(scales.astype(np.float64) - 127.0), 8, axis=1)[..., None]
    return vals.transpose(0, 1, 3, 2).reshape(g * 512, n)


K, T, J, R, C, D = 512, 2048, 256, 512, 512, 512


def setup_inputs():
    n = np.random.standard_normal
    idx = np.random.permutation(T)[:J]
    idx2 = np.random.permutation(T)[:J]
    idx3 = np.stack([np.random.permutation(C)[:J] for _ in range(8)])
    idx4 = np.stack([np.random.permutation(D)[:J] for _ in range(8)])
    fk = mx_kscale(K)
    fr = mx_kscale(R)
    xtp = pack_weight(n((K, T)) / fk[:, None], "e4m3")
    wp = pack_weight(n((K, R)) * 1 / np.sqrt(K) * fk[:, None] * fr, "e2m1")
    w2p = pack_weight(n((K, R)) * 1 / np.sqrt(K) * fk[:, None] / fr, "e5m2")
    return {
        "xt_words": xtp[0],
        "xt_scales": xtp[1],
        "w_words": wp[0],
        "w_scales": wp[1],
        "w2_words": w2p[0],
        "w2_scales": w2p[1],
        "offs": striped(idx),
        "offs2": striped(idx2),
        "offs3": striped8(idx3),
        "offs4": striped8(idx4),
    }


def reference(xt_words, xt_scales, w_words, w_scales, w2_words, w2_scales, offs, offs2, offs3, offs4):
    idx = unstriped(offs)
    idx2 = unstriped(offs2)
    idx3 = unstriped8(offs3)
    idx4 = unstriped8(offs4)
    xtu = unpack_weight(xt_words, xt_scales, "e4m3")
    wu = unpack_weight(w_words, w_scales, "e2m1")
    w2u = unpack_weight(w2_words, w2_scales, "e5m2")
    xtidxg = xtu[:, idx]
    a = wu.T @ xtidxg
    xtidx2g = xtu[:, idx2]
    b = w2u.T @ xtidx2g
    pa = np.zeros((R, C))
    pa[np.arange(R)[:, None], idx3[np.arange(R) % 512 // 64]] = a
    pb = np.zeros((R, D))
    pb[np.arange(R)[:, None], idx4[np.arange(R) % 512 // 64]] = b
    paq = mxq(pa, 0, "e4m3")
    pbq = mxq(pb, 0, "e4m3")
    p = paq.T @ pbq
    return p

@@ -1,0 +1,169 @@
+from contextlib import ExitStack
+
+import concourse.mybir as mybir
+
+K, T, J, R, C, D = 512, 2048, 256, 512, 512, 512
+FLOPS = 2 * K * R * J * 2 + 2 * R * C * D
+
+F32 = mybir.dt.float32
+BF16 = mybir.dt.bfloat16
+I32 = mybir.dt.int32
+U32 = mybir.dt.uint32
+U16 = mybir.dt.uint16
+U8 = mybir.dt.uint8
+E4M3X4 = mybir.dt.float8_e4m3fn_x4
+E5M2X4 = mybir.dt.float8_e5m2_x4
+E2M1X4 = mybir.dt.float4_e2m1fn_x4
+COPY = mybir.ActivationFunctionType.Copy
+
+P = 128
+PACK = 4
+BLOCKS = R // 32
+QUADS = 4
+HALF = D // 2
+BOARDS = 3
+
+
+def tile_list_boardsproduct_kernel(tc, xt_words, xt_scales, w_words, w_scales, w2_words, w2_scales, offs, offs2, offs3, offs4, out):
+    nc = tc.nc
+    with ExitStack() as ctx:
+        keep = ctx.enter_context(tc.tile_pool(name="keep", bufs=1))
+        psum = ctx.enter_context(tc.psum_pool(name="psum", bufs=8))
+
+        def sb(name, shape, dtype):
+            return keep.tile(shape, dtype, name=name, align_bytes=64)
+
+        lists = [sb(f"list{i}", [P, J // 16], U16) for i in range(4)]
+        x_words = sb("x_words", [P, T], U32)
+        x_bytes = sb("x_bytes", [P, T], U8)
+        w_raw = sb("w_raw", [P, R // 2], U32)
+        w2_raw = sb("w2_raw", [P, R], U32)
+        w_rows = sb("w_rows", [4, QUADS, R // 4], I32)
+        w2_rows = sb("w2_rows", [4, QUADS, R // 4], I32)
+        dealt = sb("dealt", [P, PACK * P], U32)
+        w_plane = sb("w_plane", [P, R], U8)
+        picked_words = sb("picked_words", [P, J], U32)
+        picked_bytes = sb("picked_bytes", [P, J], U8)
+
+        nc.vector.memset(x_bytes[:].bitcast(I32), 0)
+        nc.vector.memset(w_plane[:].bitcast(I32), 0)
+
+        def load_rows(rows, scales):
+            nc.sync.dma_start(out=rows[:], in_=scales[0].bitcast(I32).rearrange("(q r) c -> r q c", r=4))
+
+        nc.sync.dma_start(lists[0][:], offs)
+        nc.sync.dma_start(out=x_words[:].bitcast(I32), in_=xt_words[0].rearrange("p n t -> p (n t)").bitcast(I32))
+        load_rows(w_rows, w_scales)
+        for q in range(QUADS):
+            nc.sync.dma_start(out=x_bytes[32 * q : 32 * q + 4, :].bitcast(I32), in_=xt_scales[0, 4 * q : 4 * q + 4, :].bitcast(I32))
+        nc.sync.dma_start(out=w_raw[:].bitcast(I32), in_=w_words[0].bitcast(I32))
+        nc.sync.dma_start(lists[2][:], offs3)
+        nc.sync.dma_start(lists[1][:], offs2)
+        nc.sync.dma_start(out=w2_raw[:].bitcast(I32), in_=w2_words[0].rearrange("p n t -> p (n t)").bitcast(I32))
+        load_rows(w2_rows, w2_scales)
+        nc.sync.dma_start(lists[3][:], offs4)
+
+        boards = [[sb(f"board{s}_{i}", [P, C], F32) for i in range(BOARDS)] for s in range(2)]
+        nc.vector.memset(boards[0][0][:], 0.0)
+
+        def deal_plane(plane, rows):
+            for q in range(QUADS):
+                nc.vector.tensor_copy(
+                    out=plane[32 * q : 32 * q + 4, :].bitcast(I32).rearrange("p (t b u) -> p t b u", t=PACK, b=BLOCKS),
+                    in_=rows[:, q, :].rearrange("p (b t u) -> p t b u", t=PACK, b=BLOCKS),
+                )
+
+        def gather(offsets):
+            nc.vector.tensor_copy(picked_words[:], x_words[:].indirect(offsets[:]))
+            nc.vector.tensor_copy(picked_bytes[:], x_bytes[:].indirect(offsets[:]))
+
+        def first_stage(width, dtype):
+            sums = []
+            for t in range(PACK):
+                acc = psum.tile([P, J], F32, name="acc")
+                nc.tensor.matmul_mx(
+                    out=acc[:],
+                    lhsT=dealt[:, t * width : (t + 1) * width].bitcast(dtype),
+                    lhsT_scale=w_plane[:, t * P : (t + 1) * P],
+                    rhs=picked_words[:].bitcast(E4M3X4),
+                    rhs_scale=picked_bytes[:],
+                    start=True,
+                    stop=True,
+                )
+                sums.append(acc)
+            return sums
+
+        def fetch(name, sums):
+            results = [sb(f"{name}{t}", [P, J], F32) for t in range(len(sums))]
+            for res, acc in zip(results, sums):
+                nc.vector.tensor_copy(out=res[:], in_=acc[:])
+            return results
+
+        deal_plane(w_plane, w_rows)
+        nc.scalar.copy(
+            out=dealt[:, : R // 2].rearrange("p (t b u) -> p t b u", t=PACK, b=BLOCKS),
+            in_=w_raw[:].rearrange("p (b t u) -> p t b u", t=PACK, b=BLOCKS),
+        )
+        gather(lists[0])
+        a_sums = first_stage(P // 2, E2M1X4)
+        a = fetch("a", a_sums[: PACK - 1])
+
+        for board in boards[0][1:] + boards[1]:
+            nc.vector.memset(board[:], 0.0)
+        gather(lists[1])
+        deal_plane(w_plane, w2_rows)
+        nc.vector.tensor_copy(
+            out=dealt[:].rearrange("p (t b u) -> p t b u", t=PACK, b=BLOCKS),
+            in_=w2_raw[:].rearrange("p (b t u) -> p t b u", t=PACK, b=BLOCKS),
+        )
+        b = fetch("b", first_stage(P, E5M2X4))
+
+        pa_woven = [sb(f"pa_woven{m}", [P, P, PACK], BF16) for m in range(C // P)]
+        pb_woven = sb("pb_woven", [P, D, PACK], BF16)
+
+        def scatter(side, t, values):
+            board = boards[side][t % BOARDS]
+            nc.scalar.activation(out=board[:].indirect(lists[2 + side][:]), in_=values[:], func=COPY)
+            return board
+
+        for t in range(PACK - 1):
+            board = scatter(0, t, a[t])
+            for m in range(C // P):
+                nc.vector.tensor_copy(out=pa_woven[m][:, :, t], in_=board[:, m * P : (m + 1) * P])
+        for t in range(PACK):
+            board = scatter(1, t, b[t])
+            if t == PACK - 2:
+                nc.vector.tensor_copy(out=b[t][:], in_=a_sums[PACK - 1][:])
+            nc.vector.tensor_copy(out=pb_woven[:, :, t], in_=board[:])
+        pb_codes = sb("pb_codes", [P, D], U32)
+        pb_plane = sb("pb_plane", [P, D], U8)
+        nc.vector.quantize_mx(out=pb_codes[:].bitcast(E4M3X4), scales=pb_plane[:], in_=pb_woven[:].rearrange("p d t -> p (d t)"))
+
+        board = scatter(0, PACK - 1, b[PACK - 2])
+        for m in range(C // P):
+            nc.vector.tensor_copy(out=pa_woven[m][:, :, PACK - 1], in_=board[:, m * P : (m + 1) * P])
+            codes = sb(f"pa_codes{m}", [P, P], U32)
+            plane = sb(f"pa_plane{m}", [P, P], U8)
+            nc.vector.quantize_mx(out=codes[:].bitcast(E4M3X4), scales=plane[:], in_=pa_woven[m][:].rearrange("p c t -> p (c t)"))
+            res = sb(f"res{m}", [P, D], F32)
+            rows = slice(m * P, (m + 1) * P)
+            for h in range(2):
+                cols = slice(h * HALF, (h + 1) * HALF)
+                acc = psum.tile([P, HALF], F32, name="acc")
+                nc.tensor.matmul_mx(
+                    out=acc[:],
+                    lhsT=codes[:].bitcast(E4M3X4),
+                    lhsT_scale=plane[:],
+                    rhs=pb_codes[:, cols].bitcast(E4M3X4),
+                    rhs_scale=pb_plane[:, cols],
+                    start=True,
+                    stop=True,
+                )
+                if m >= 2 and h == 1:
+                    nc.vector.tensor_copy(out=res[:, cols], in_=acc[:])
+                else:
+                    nc.scalar.copy(out=res[:, cols], in_=acc[:])
+                if m == 0:
+                    nc.sync.dma_start(out=out[rows, cols], in_=res[:, cols])
+            if m > 0:
+                nc.sync.dma_start(out=out[rows, :], in_=res[:])

@@ -21,7 +21,7 @@ PACK = 4
 BLOCKS = R // 32
 QUADS = 4
 HALF = D // 2
-BOARDS = 3
+A_BOARDS, B_BOARDS = 2, 3
 
 
 def tile_list_boardsproduct_kernel(tc, xt_words, xt_scales, w_words, w_scales, w2_words, w2_scales, offs, offs2, offs3, offs4, out):
@@ -33,38 +33,40 @@ def tile_list_boardsproduct_kernel(tc, xt_words, xt_scales, w_words, w_scales, w
         def sb(name, shape, dtype):
             return keep.tile(shape, dtype, name=name, align_bytes=64)
 
-        lists = [sb(f"list{i}", [P, J // 16], U16) for i in range(4)]
+        list1, list2, list3, list4 = [sb(f"list{i}", [P, J // 16], U16) for i in range(4)]
         x_words = sb("x_words", [P, T], U32)
         x_bytes = sb("x_bytes", [P, T], U8)
         w_raw = sb("w_raw", [P, R // 2], U32)
         w2_raw = sb("w2_raw", [P, R], U32)
         w_rows = sb("w_rows", [4, QUADS, R // 4], I32)
         w2_rows = sb("w2_rows", [4, QUADS, R // 4], I32)
-        dealt = sb("dealt", [P, PACK * P], U32)
+        w_dealt = sb("w_dealt", [P, PACK, P // 2], U32)
+        w2_dealt = [sb("w2_dealt_first", [P, 1, P], U32), sb("w2_dealt_rest", [P, PACK - 1, P], U32)]
         w_plane = sb("w_plane", [P, R], U8)
-        picked_words = sb("picked_words", [P, J], U32)
-        picked_bytes = sb("picked_bytes", [P, J], U8)
+        w2_plane = sb("w2_plane", [P, R], U8)
+        a_boards = [sb(f"a_board{i}", [P, C], F32) for i in range(A_BOARDS)]
+        b_boards = [sb(f"b_board{i}", [P, D], F32) for i in range(B_BOARDS)]
 
         nc.vector.memset(x_bytes[:].bitcast(I32), 0)
+        nc.vector.memset(w2_plane[:].bitcast(I32), 0)
         nc.vector.memset(w_plane[:].bitcast(I32), 0)
+        for board in b_boards + a_boards:
+            nc.vector.memset(board[:], 0.0)
 
         def load_rows(rows, scales):
             nc.sync.dma_start(out=rows[:], in_=scales[0].bitcast(I32).rearrange("(q r) c -> r q c", r=4))
 
-        nc.sync.dma_start(lists[0][:], offs)
+        nc.sync.dma_start(list2[:], offs2)
+        load_rows(w2_rows, w2_scales)
         nc.sync.dma_start(out=x_words[:].bitcast(I32), in_=xt_words[0].rearrange("p n t -> p (n t)").bitcast(I32))
-        load_rows(w_rows, w_scales)
         for q in range(QUADS):
             nc.sync.dma_start(out=x_bytes[32 * q : 32 * q + 4, :].bitcast(I32), in_=xt_scales[0, 4 * q : 4 * q + 4, :].bitcast(I32))
-        nc.sync.dma_start(out=w_raw[:].bitcast(I32), in_=w_words[0].bitcast(I32))
-        nc.sync.dma_start(lists[2][:], offs3)
-        nc.sync.dma_start(lists[1][:], offs2)
         nc.sync.dma_start(out=w2_raw[:].bitcast(I32), in_=w2_words[0].rearrange("p n t -> p (n t)").bitcast(I32))
-        load_rows(w2_rows, w2_scales)
-        nc.sync.dma_start(lists[3][:], offs4)
-
-        boards = [[sb(f"board{s}_{i}", [P, C], F32) for i in range(BOARDS)] for s in range(2)]
-        nc.vector.memset(boards[0][0][:], 0.0)
+        nc.sync.dma_start(list4[:], offs4)
+        nc.sync.dma_start(list1[:], offs)
+        nc.sync.dma_start(out=w_raw[:].bitcast(I32), in_=w_words[0].bitcast(I32))
+        load_rows(w_rows, w_scales)
+        nc.sync.dma_start(list3[:], offs3)
 
         def deal_plane(plane, rows):
             for q in range(QUADS):
@@ -73,75 +75,65 @@ def tile_list_boardsproduct_kernel(tc, xt_words, xt_scales, w_words, w_scales, w
                     in_=rows[:, q, :].rearrange("p (b t u) -> p t b u", t=PACK, b=BLOCKS),
                 )
 
-        def gather(offsets):
-            nc.vector.tensor_copy(picked_words[:], x_words[:].indirect(offsets[:]))
-            nc.vector.tensor_copy(picked_bytes[:], x_bytes[:].indirect(offsets[:]))
+        def gather(name, offsets):
+            words = sb(name + "_words", [P, J], U32)
+            scale_bytes = sb(name + "_bytes", [P, J], U8)
+            nc.vector.tensor_copy(words[:], x_words[:].indirect(offsets[:]))
+            nc.vector.tensor_copy(scale_bytes[:], x_bytes[:].indirect(offsets[:]))
+            return words, scale_bytes
 
-        def first_stage(width, dtype):
-            sums = []
-            for t in range(PACK):
-                acc = psum.tile([P, J], F32, name="acc")
-                nc.tensor.matmul_mx(
-                    out=acc[:],
-                    lhsT=dealt[:, t * width : (t + 1) * width].bitcast(dtype),
-                    lhsT_scale=w_plane[:, t * P : (t + 1) * P],
-                    rhs=picked_words[:].bitcast(E4M3X4),
-                    rhs_scale=picked_bytes[:],
-                    start=True,
-                    stop=True,
-                )
-                sums.append(acc)
-            return sums
+        def first_product(name, codes, plane, picked, fetch):
+            words, scale_bytes = picked
+            acc = psum.tile([P, J], F32, name="acc")
+            nc.tensor.matmul_mx(out=acc[:], lhsT=codes, lhsT_scale=plane, rhs=words[:].bitcast(E4M3X4), rhs_scale=scale_bytes[:], start=True, stop=True)
+            res = sb(name, [P, J], F32)
+            fetch(out=res[:], in_=acc[:])
+            return res
 
-        def fetch(name, sums):
-            results = [sb(f"{name}{t}", [P, J], F32) for t in range(len(sums))]
-            for res, acc in zip(results, sums):
-                nc.vector.tensor_copy(out=res[:], in_=acc[:])
-            return results
+        deal_plane(w2_plane, w2_rows)
+        picked_b = gather("xb", list2)
+        w2_by_t = w2_raw[:].rearrange("p (b t u) -> p t b u", t=PACK, b=BLOCKS)
+        nc.scalar.copy(out=w2_dealt[0][:].rearrange("p t (b u) -> p t b u", b=BLOCKS), in_=w2_by_t[:, :1])
+        nc.scalar.copy(out=w2_dealt[1][:].rearrange("p t (b u) -> p t b u", b=BLOCKS), in_=w2_by_t[:, 1:])
+        w2_slices = [w2_dealt[0][:, 0, :]] + [w2_dealt[1][:, t, :] for t in range(PACK - 1)]
+        b = [
+            first_product(f"b{t}", w2_slices[t].bitcast(E5M2X4), w2_plane[:, t * P : (t + 1) * P], picked_b, nc.scalar.copy if t == 0 else nc.vector.tensor_copy)
+            for t in range(PACK)
+        ]
 
+        picked_a = gather("xa", list1)
         deal_plane(w_plane, w_rows)
-        nc.scalar.copy(
-            out=dealt[:, : R // 2].rearrange("p (t b u) -> p t b u", t=PACK, b=BLOCKS),
+        nc.vector.tensor_copy(
+            out=w_dealt[:].rearrange("p t (b u) -> p t b u", b=BLOCKS),
             in_=w_raw[:].rearrange("p (b t u) -> p t b u", t=PACK, b=BLOCKS),
         )
-        gather(lists[0])
-        a_sums = first_stage(P // 2, E2M1X4)
-        a = fetch("a", a_sums[: PACK - 1])
+        a = [
+            first_product(f"a{t}", w_dealt[:, t, :].bitcast(E2M1X4), w_plane[:, t * P : (t + 1) * P], picked_a, nc.vector.tensor_copy)
+            for t in range(PACK)
+        ]
 
-        for board in boards[0][1:] + boards[1]:
-            nc.vector.memset(board[:], 0.0)
-        gather(lists[1])
-        deal_plane(w_plane, w2_rows)
-        nc.vector.tensor_copy(
-            out=dealt[:].rearrange("p (t b u) -> p t b u", t=PACK, b=BLOCKS),
-            in_=w2_raw[:].rearrange("p (b t u) -> p t b u", t=PACK, b=BLOCKS),
-        )
-        b = fetch("b", first_stage(P, E5M2X4))
-
-        pa_woven = [sb(f"pa_woven{m}", [P, P, PACK], BF16) for m in range(C // P)]
         pb_woven = sb("pb_woven", [P, D, PACK], BF16)
-
-        def scatter(side, t, values):
-            board = boards[side][t % BOARDS]
-            nc.scalar.activation(out=board[:].indirect(lists[2 + side][:]), in_=values[:], func=COPY)
-            return board
-
-        for t in range(PACK - 1):
-            board = scatter(0, t, a[t])
-            for m in range(C // P):
-                nc.vector.tensor_copy(out=pa_woven[m][:, :, t], in_=board[:, m * P : (m + 1) * P])
         for t in range(PACK):
-            board = scatter(1, t, b[t])
-            if t == PACK - 2:
-                nc.vector.tensor_copy(out=b[t][:], in_=a_sums[PACK - 1][:])
+            board = b_boards[t % B_BOARDS]
+            nc.scalar.activation(out=board[:].indirect(list4[:]), in_=b[t][:], func=COPY)
             nc.vector.tensor_copy(out=pb_woven[:, :, t], in_=board[:])
         pb_codes = sb("pb_codes", [P, D], U32)
         pb_plane = sb("pb_plane", [P, D], U8)
         nc.vector.quantize_mx(out=pb_codes[:].bitcast(E4M3X4), scales=pb_plane[:], in_=pb_woven[:].rearrange("p d t -> p (d t)"))
 
-        board = scatter(0, PACK - 1, b[PACK - 2])
+        pa_woven = [sb(f"pa_woven{m}", [P, P, PACK], BF16) for m in range(C // P)]
+
+        def weave_a(t, m):
+            nc.vector.tensor_copy(out=pa_woven[m][:, :, t], in_=a_boards[t % A_BOARDS][:, m * P : (m + 1) * P])
+
+        for t in range(PACK):
+            nc.scalar.activation(out=a_boards[t % A_BOARDS][:].indirect(list3[:]), in_=a[t][:], func=COPY)
+            if t < PACK - 1:
+                for m in range(C // P):
+                    weave_a(t, m)
+
         for m in range(C // P):
-            nc.vector.tensor_copy(out=pa_woven[m][:, :, PACK - 1], in_=board[:, m * P : (m + 1) * P])
+            weave_a(PACK - 1, m)
             codes = sb(f"pa_codes{m}", [P, P], U32)
             plane = sb(f"pa_plane{m}", [P, P], U8)
             nc.vector.quantize_mx(out=codes[:].bitcast(E4M3X4), scales=plane[:], in_=pa_woven[m][:].rearrange("p c t -> p (c t)"))
@@ -163,7 +155,7 @@ def tile_list_boardsproduct_kernel(tc, xt_words, xt_scales, w_words, w_scales, w
                     nc.vector.tensor_copy(out=res[:, cols], in_=acc[:])
                 else:
                     nc.scalar.copy(out=res[:, cols], in_=acc[:])
-                if m == 0:
+                if m in (0, 3):
                     nc.sync.dma_start(out=out[rows, cols], in_=res[:, cols])
-            if m > 0:
+            if m in (1, 2):
                 nc.sync.dma_start(out=out[rows, :], in_=res[:])

@@ -21,7 +21,7 @@ PACK = 4
 BLOCKS = R // 32
 QUADS = 4
 HALF = D // 2
-A_BOARDS, B_BOARDS = 2, 3
+A_BOARDS, B_BOARDS = 2, 4
 
 
 def tile_list_boardsproduct_kernel(tc, xt_words, xt_scales, w_words, w_scales, w2_words, w2_scales, offs, offs2, offs3, offs4, out):
@@ -30,8 +30,8 @@ def tile_list_boardsproduct_kernel(tc, xt_words, xt_scales, w_words, w_scales, w
         keep = ctx.enter_context(tc.tile_pool(name="keep", bufs=1))
         psum = ctx.enter_context(tc.psum_pool(name="psum", bufs=8))
 
-        def sb(name, shape, dtype):
-            return keep.tile(shape, dtype, name=name, align_bytes=64)
+        def sb(name, shape, dtype, tag=None):
+            return keep.tile(shape, dtype, name=name, tag=tag or name, align_bytes=64)
 
         list1, list2, list3, list4 = [sb(f"list{i}", [P, J // 16], U16) for i in range(4)]
         x_words = sb("x_words", [P, T], U32)
@@ -50,22 +50,24 @@ def tile_list_boardsproduct_kernel(tc, xt_words, xt_scales, w_words, w_scales, w
         nc.vector.memset(x_bytes[:].bitcast(I32), 0)
         nc.vector.memset(w2_plane[:].bitcast(I32), 0)
         nc.vector.memset(w_plane[:].bitcast(I32), 0)
-        for board in b_boards + a_boards:
+        for board in b_boards:
             nc.vector.memset(board[:], 0.0)
+        for board in a_boards:
+            nc.gpsimd.memset(board[:], 0.0)
 
-        def load_rows(rows, scales):
-            nc.sync.dma_start(out=rows[:], in_=scales[0].bitcast(I32).rearrange("(q r) c -> r q c", r=4))
+        def load_rows(queue, rows, scales):
+            queue.dma_start(out=rows[:], in_=scales[0].bitcast(I32).rearrange("(q r) c -> r q c", r=4))
 
+        load_rows(nc.scalar, w2_rows, w2_scales)
         nc.sync.dma_start(list2[:], offs2)
-        load_rows(w2_rows, w2_scales)
         nc.sync.dma_start(out=x_words[:].bitcast(I32), in_=xt_words[0].rearrange("p n t -> p (n t)").bitcast(I32))
         for q in range(QUADS):
             nc.sync.dma_start(out=x_bytes[32 * q : 32 * q + 4, :].bitcast(I32), in_=xt_scales[0, 4 * q : 4 * q + 4, :].bitcast(I32))
         nc.sync.dma_start(out=w2_raw[:].bitcast(I32), in_=w2_words[0].rearrange("p n t -> p (n t)").bitcast(I32))
         nc.sync.dma_start(list4[:], offs4)
         nc.sync.dma_start(list1[:], offs)
+        load_rows(nc.sync, w_rows, w_scales)
         nc.sync.dma_start(out=w_raw[:].bitcast(I32), in_=w_words[0].bitcast(I32))
-        load_rows(w_rows, w_scales)
         nc.sync.dma_start(list3[:], offs3)
 
         def deal_plane(plane, rows):
@@ -82,12 +84,14 @@ def tile_list_boardsproduct_kernel(tc, xt_words, xt_scales, w_words, w_scales, w
             nc.vector.tensor_copy(scale_bytes[:], x_bytes[:].indirect(offsets[:]))
             return words, scale_bytes
 
-        def first_product(name, codes, plane, picked, fetch):
+        def first_product(name, codes, plane, picked, fetch, width):
             words, scale_bytes = picked
-            acc = psum.tile([P, J], F32, name="acc")
-            nc.tensor.matmul_mx(out=acc[:], lhsT=codes, lhsT_scale=plane, rhs=words[:].bitcast(E4M3X4), rhs_scale=scale_bytes[:], start=True, stop=True)
             res = sb(name, [P, J], F32)
-            fetch(out=res[:], in_=acc[:])
+            for j0 in range(0, J, width):
+                cols = slice(j0, j0 + width)
+                acc = psum.tile([P, width], F32, name="acc")
+                nc.tensor.matmul_mx(out=acc[:], lhsT=codes, lhsT_scale=plane, rhs=words[:, cols].bitcast(E4M3X4), rhs_scale=scale_bytes[:, cols], start=True, stop=True)
+                fetch(out=res[:, cols], in_=acc[:])
             return res
 
         deal_plane(w2_plane, w2_rows)
@@ -97,7 +101,7 @@ def tile_list_boardsproduct_kernel(tc, xt_words, xt_scales, w_words, w_scales, w
         nc.scalar.copy(out=w2_dealt[1][:].rearrange("p t (b u) -> p t b u", b=BLOCKS), in_=w2_by_t[:, 1:])
         w2_slices = [w2_dealt[0][:, 0, :]] + [w2_dealt[1][:, t, :] for t in range(PACK - 1)]
         b = [
-            first_product(f"b{t}", w2_slices[t].bitcast(E5M2X4), w2_plane[:, t * P : (t + 1) * P], picked_b, nc.scalar.copy if t == 0 else nc.vector.tensor_copy)
+            first_product(f"b{t}", w2_slices[t].bitcast(E5M2X4), w2_plane[:, t * P : (t + 1) * P], picked_b, nc.scalar.copy if t == 0 else nc.vector.tensor_copy, J // 2 if t == 0 else J)
             for t in range(PACK)
         ]
 
@@ -108,11 +112,11 @@ def tile_list_boardsproduct_kernel(tc, xt_words, xt_scales, w_words, w_scales, w
             in_=w_raw[:].rearrange("p (b t u) -> p t b u", t=PACK, b=BLOCKS),
         )
         a = [
-            first_product(f"a{t}", w_dealt[:, t, :].bitcast(E2M1X4), w_plane[:, t * P : (t + 1) * P], picked_a, nc.vector.tensor_copy)
+            first_product(f"a{t}", w_dealt[:, t, :].bitcast(E2M1X4), w_plane[:, t * P : (t + 1) * P], picked_a, nc.vector.tensor_copy, J)
             for t in range(PACK)
         ]
 
-        pb_woven = sb("pb_woven", [P, D, PACK], BF16)
+        pb_woven = sb("pb_woven", [P, D, PACK], BF16, tag="w_raw")
         for t in range(PACK):
             board = b_boards[t % B_BOARDS]
             nc.scalar.activation(out=board[:].indirect(list4[:]), in_=b[t][:], func=COPY)
@@ -139,9 +143,11 @@ def tile_list_boardsproduct_kernel(tc, xt_words, xt_scales, w_words, w_scales, w
             nc.vector.quantize_mx(out=codes[:].bitcast(E4M3X4), scales=plane[:], in_=pa_woven[m][:].rearrange("p c t -> p (c t)"))
             res = sb(f"res{m}", [P, D], F32)
             rows = slice(m * P, (m + 1) * P)
-            for h in range(2):
-                cols = slice(h * HALF, (h + 1) * HALF)
-                acc = psum.tile([P, HALF], F32, name="acc")
+            last = m == C // P - 1
+            edges = (0, HALF, HALF + HALF // 2, D) if last else (0, HALF, D)
+            for h in range(len(edges) - 1):
+                cols = slice(edges[h], edges[h + 1])
+                acc = psum.tile([P, edges[h + 1] - edges[h]], F32, name="acc")
                 nc.tensor.matmul_mx(
                     out=acc[:],
                     lhsT=codes[:].bitcast(E4M3X4),
@@ -155,7 +161,8 @@ def tile_list_boardsproduct_kernel(tc, xt_words, xt_scales, w_words, w_scales, w
                     nc.vector.tensor_copy(out=res[:, cols], in_=acc[:])
                 else:
                     nc.scalar.copy(out=res[:, cols], in_=acc[:])
-                if m in (0, 3):
-                    nc.sync.dma_start(out=out[rows, cols], in_=res[:, cols])
-            if m in (1, 2):
+            if m in (0, 3):
+                nc.sync.dma_start(out=out[rows, :HALF], in_=res[:, :HALF])
+                nc.sync.dma_start(out=out[rows, HALF:], in_=res[:, HALF:])
+            else:
                 nc.sync.dma_start(out=out[rows, :], in_=res[:])

@@ -20,34 +20,40 @@ P = 128
 PACK = 4
 BLOCKS = R // 32
 QUADS = 4
-HALF = D // 2
-A_BOARDS, B_BOARDS = 2, 4
+LIVE = 4
+BANKS = 8
+C_TILES = C // P
+HALF, QUARTER = D // 2, D // 4
+A_BOARDS = 2
+DIRECT = 2
+RUN = 4
 
 
 def tile_list_boardsproduct_kernel(tc, xt_words, xt_scales, w_words, w_scales, w2_words, w2_scales, offs, offs2, offs3, offs4, out):
     nc = tc.nc
     with ExitStack() as ctx:
         keep = ctx.enter_context(tc.tile_pool(name="keep", bufs=1))
-        psum = ctx.enter_context(tc.psum_pool(name="psum", bufs=8))
+        psum = ctx.enter_context(tc.psum_pool(name="psum", bufs=BANKS))
 
         def sb(name, shape, dtype, tag=None):
             return keep.tile(shape, dtype, name=name, tag=tag or name, align_bytes=64)
 
         list1, list2, list3, list4 = [sb(f"list{i}", [P, J // 16], U16) for i in range(4)]
         x_words = sb("x_words", [P, T], U32)
-        x_bytes = sb("x_bytes", [P, T], U8)
+        x_plane = sb("x_plane", [P, T], U8)
         w_raw = sb("w_raw", [P, R // 2], U32)
         w2_raw = sb("w2_raw", [P, R], U32)
-        w_rows = sb("w_rows", [4, QUADS, R // 4], I32)
-        w2_rows = sb("w2_rows", [4, QUADS, R // 4], I32)
+        w_rows = sb("w_rows", [LIVE, QUADS, R // 4], I32)
+        w2_rows = sb("w2_rows", [LIVE, QUADS, R // 4], I32)
         w_dealt = sb("w_dealt", [P, PACK, P // 2], U32)
-        w2_dealt = [sb("w2_dealt_first", [P, 1, P], U32), sb("w2_dealt_rest", [P, PACK - 1, P], U32)]
+        w2_dealt_first = sb("w2_dealt_first", [P, 1, P], U32)
+        w2_dealt_rest = sb("w2_dealt_rest", [P, PACK - 1, P], U32)
         w_plane = sb("w_plane", [P, R], U8)
         w2_plane = sb("w2_plane", [P, R], U8)
         a_boards = [sb(f"a_board{i}", [P, C], F32) for i in range(A_BOARDS)]
-        b_boards = [sb(f"b_board{i}", [P, D], F32) for i in range(B_BOARDS)]
+        b_boards = [sb(f"b_board{t}", [P, D], F32) for t in range(PACK)]
 
-        nc.vector.memset(x_bytes[:].bitcast(I32), 0)
+        nc.vector.memset(x_plane[:].bitcast(I32), 0)
         nc.vector.memset(w2_plane[:].bitcast(I32), 0)
         nc.vector.memset(w_plane[:].bitcast(I32), 0)
         for board in b_boards:
@@ -56,13 +62,13 @@ def tile_list_boardsproduct_kernel(tc, xt_words, xt_scales, w_words, w_scales, w
             nc.gpsimd.memset(board[:], 0.0)
 
         def load_rows(queue, rows, scales):
-            queue.dma_start(out=rows[:], in_=scales[0].bitcast(I32).rearrange("(q r) c -> r q c", r=4))
+            queue.dma_start(out=rows[:], in_=scales[0].bitcast(I32).rearrange("(g i) c -> i g c", i=LIVE))
 
         load_rows(nc.scalar, w2_rows, w2_scales)
         nc.sync.dma_start(list2[:], offs2)
         nc.sync.dma_start(out=x_words[:].bitcast(I32), in_=xt_words[0].rearrange("p n t -> p (n t)").bitcast(I32))
-        for q in range(QUADS):
-            nc.sync.dma_start(out=x_bytes[32 * q : 32 * q + 4, :].bitcast(I32), in_=xt_scales[0, 4 * q : 4 * q + 4, :].bitcast(I32))
+        for i in range(LIVE):
+            nc.sync.dma_start(out=x_plane[i:P:32, :].bitcast(I32), in_=xt_scales[0, i : QUADS * LIVE : LIVE, :].bitcast(I32))
         nc.sync.dma_start(out=w2_raw[:].bitcast(I32), in_=w2_words[0].rearrange("p n t -> p (n t)").bitcast(I32))
         nc.sync.dma_start(list4[:], offs4)
         nc.sync.dma_start(list1[:], offs)
@@ -70,47 +76,56 @@ def tile_list_boardsproduct_kernel(tc, xt_words, xt_scales, w_words, w_scales, w
         nc.sync.dma_start(out=w_raw[:].bitcast(I32), in_=w_words[0].bitcast(I32))
         nc.sync.dma_start(list3[:], offs3)
 
+        def by_slice(columns):
+            return columns.rearrange("p (n t u) -> p t n u", t=PACK, n=BLOCKS)
+
         def deal_plane(plane, rows):
-            for q in range(QUADS):
+            for g in range(QUADS):
                 nc.vector.tensor_copy(
-                    out=plane[32 * q : 32 * q + 4, :].bitcast(I32).rearrange("p (t b u) -> p t b u", t=PACK, b=BLOCKS),
-                    in_=rows[:, q, :].rearrange("p (b t u) -> p t b u", t=PACK, b=BLOCKS),
+                    out=plane[32 * g : 32 * g + LIVE, :].bitcast(I32).rearrange("p (t n u) -> p t n u", t=PACK, n=BLOCKS),
+                    in_=by_slice(rows[:, g, :]),
                 )
+
+        def deal_words(copy, dealt, raw_by_slice):
+            copy(out=dealt[:].rearrange("p t (n u) -> p t n u", n=BLOCKS), in_=raw_by_slice)
 
         def gather(name, offsets):
             words = sb(name + "_words", [P, J], U32)
-            scale_bytes = sb(name + "_bytes", [P, J], U8)
+            plane = sb(name + "_plane", [P, J], U8)
             nc.vector.tensor_copy(words[:], x_words[:].indirect(offsets[:]))
-            nc.vector.tensor_copy(scale_bytes[:], x_bytes[:].indirect(offsets[:]))
-            return words, scale_bytes
+            nc.vector.tensor_copy(plane[:], x_plane[:].indirect(offsets[:]))
+            return words, plane
 
         def first_product(name, codes, plane, picked, fetch, width):
-            words, scale_bytes = picked
-            res = sb(name, [P, J], F32)
+            picked_words, picked_plane = picked
+            values = sb(name, [P, J], F32)
             for j0 in range(0, J, width):
-                cols = slice(j0, j0 + width)
+                slots = slice(j0, j0 + width)
                 acc = psum.tile([P, width], F32, name="acc")
-                nc.tensor.matmul_mx(out=acc[:], lhsT=codes, lhsT_scale=plane, rhs=words[:, cols].bitcast(E4M3X4), rhs_scale=scale_bytes[:, cols], start=True, stop=True)
-                fetch(out=res[:, cols], in_=acc[:])
-            return res
+                nc.tensor.matmul_mx(
+                    out=acc[:],
+                    lhsT=codes,
+                    lhsT_scale=plane,
+                    rhs=picked_words[:, slots].bitcast(E4M3X4),
+                    rhs_scale=picked_plane[:, slots],
+                    start=True,
+                    stop=True,
+                )
+                fetch(out=values[:, slots], in_=acc[:])
+            return values
 
         deal_plane(w2_plane, w2_rows)
         picked_b = gather("xb", list2)
-        w2_by_t = w2_raw[:].rearrange("p (b t u) -> p t b u", t=PACK, b=BLOCKS)
-        nc.scalar.copy(out=w2_dealt[0][:].rearrange("p t (b u) -> p t b u", b=BLOCKS), in_=w2_by_t[:, :1])
-        nc.scalar.copy(out=w2_dealt[1][:].rearrange("p t (b u) -> p t b u", b=BLOCKS), in_=w2_by_t[:, 1:])
-        w2_slices = [w2_dealt[0][:, 0, :]] + [w2_dealt[1][:, t, :] for t in range(PACK - 1)]
-        b = [
-            first_product(f"b{t}", w2_slices[t].bitcast(E5M2X4), w2_plane[:, t * P : (t + 1) * P], picked_b, nc.scalar.copy if t == 0 else nc.vector.tensor_copy, J // 2 if t == 0 else J)
-            for t in range(PACK)
-        ]
+        deal_words(nc.scalar.copy, w2_dealt_first, by_slice(w2_raw[:])[:, :1])
+        deal_words(nc.scalar.copy, w2_dealt_rest, by_slice(w2_raw[:])[:, 1:])
+        b = [first_product("b0", w2_dealt_first[:, 0, :].bitcast(E5M2X4), w2_plane[:, :P], picked_b, nc.scalar.copy, J // 2)]
+        for t in range(1, PACK):
+            codes = w2_dealt_rest[:, t - 1, :].bitcast(E5M2X4)
+            b.append(first_product(f"b{t}", codes, w2_plane[:, t * P : (t + 1) * P], picked_b, nc.vector.tensor_copy, J))
 
         picked_a = gather("xa", list1)
         deal_plane(w_plane, w_rows)
-        nc.vector.tensor_copy(
-            out=w_dealt[:].rearrange("p t (b u) -> p t b u", b=BLOCKS),
-            in_=w_raw[:].rearrange("p (b t u) -> p t b u", t=PACK, b=BLOCKS),
-        )
+        deal_words(nc.vector.tensor_copy, w_dealt, by_slice(w_raw[:]))
         a = [
             first_product(f"a{t}", w_dealt[:, t, :].bitcast(E2M1X4), w_plane[:, t * P : (t + 1) * P], picked_a, nc.vector.tensor_copy, J)
             for t in range(PACK)
@@ -118,51 +133,60 @@ def tile_list_boardsproduct_kernel(tc, xt_words, xt_scales, w_words, w_scales, w
 
         pb_woven = sb("pb_woven", [P, D, PACK], BF16, tag="w_raw")
         for t in range(PACK):
-            board = b_boards[t % B_BOARDS]
-            nc.scalar.activation(out=board[:].indirect(list4[:]), in_=b[t][:], func=COPY)
-            nc.vector.tensor_copy(out=pb_woven[:, :, t], in_=board[:])
+            nc.scalar.activation(out=b_boards[t][:].indirect(list4[:]), in_=b[t][:], func=COPY)
+            nc.vector.tensor_copy(out=pb_woven[:, :, t], in_=b_boards[t][:])
         pb_codes = sb("pb_codes", [P, D], U32)
         pb_plane = sb("pb_plane", [P, D], U8)
         nc.vector.quantize_mx(out=pb_codes[:].bitcast(E4M3X4), scales=pb_plane[:], in_=pb_woven[:].rearrange("p d t -> p (d t)"))
 
-        pa_woven = [sb(f"pa_woven{m}", [P, P, PACK], BF16) for m in range(C // P)]
+        pa_woven = [sb(f"pa_woven{m}", [P, P, PACK], BF16) for m in range(DIRECT)]
+        pa_planar = sb("pa_planar", [P, PACK, C - DIRECT * P], BF16)
 
-        def weave_a(t, m):
+        def weave_direct(t, m):
             nc.vector.tensor_copy(out=pa_woven[m][:, :, t], in_=a_boards[t % A_BOARDS][:, m * P : (m + 1) * P])
 
         for t in range(PACK):
-            nc.scalar.activation(out=a_boards[t % A_BOARDS][:].indirect(list3[:]), in_=a[t][:], func=COPY)
+            board = a_boards[t % A_BOARDS]
+            nc.scalar.activation(out=board[:].indirect(list3[:]), in_=a[t][:], func=COPY)
             if t < PACK - 1:
-                for m in range(C // P):
-                    weave_a(t, m)
+                for m in range(DIRECT):
+                    weave_direct(t, m)
+                nc.vector.tensor_copy(out=pa_planar[:, t, :], in_=board[:, DIRECT * P :])
+            else:
+                nc.scalar.copy(out=pa_planar[:, t, :], in_=board[:, DIRECT * P :])
 
-        for m in range(C // P):
-            weave_a(PACK - 1, m)
-            codes = sb(f"pa_codes{m}", [P, P], U32)
-            plane = sb(f"pa_plane{m}", [P, P], U8)
-            nc.vector.quantize_mx(out=codes[:].bitcast(E4M3X4), scales=plane[:], in_=pa_woven[m][:].rearrange("p c t -> p (c t)"))
-            res = sb(f"res{m}", [P, D], F32)
-            rows = slice(m * P, (m + 1) * P)
-            last = m == C // P - 1
-            edges = (0, HALF, HALF + HALF // 2, D) if last else (0, HALF, D)
-            for h in range(len(edges) - 1):
-                cols = slice(edges[h], edges[h + 1])
-                acc = psum.tile([P, edges[h + 1] - edges[h]], F32, name="acc")
+        for m in range(C_TILES):
+            woven = pa_woven[m % DIRECT]
+            if m < DIRECT:
+                weave_direct(PACK - 1, m)
+            else:
+                nc.vector.tensor_copy(
+                    out=woven[:].rearrange("p (c i) t -> p c t i", i=RUN),
+                    in_=pa_planar[:, :, (m - DIRECT) * P : (m - DIRECT + 1) * P].rearrange("p t (c i) -> p c t i", i=RUN),
+                )
+            pa_codes = sb(f"pa_codes{m}", [P, P], U32)
+            pa_plane = sb(f"pa_plane{m}", [P, P], U8)
+            nc.vector.quantize_mx(out=pa_codes[:].bitcast(E4M3X4), scales=pa_plane[:], in_=woven[:].rearrange("p c t -> p (c t)"))
+
+            store_edges = (0, QUARTER, HALF, D) if m == 0 else (0, HALF, D)
+            sum_edges = (0, HALF, HALF + QUARTER, D) if m == C_TILES - 1 else store_edges
+            result = sb(f"result{m}", [P, D], F32)
+            for h in range(len(sum_edges) - 1):
+                cols = slice(sum_edges[h], sum_edges[h + 1])
+                acc = psum.tile([P, cols.stop - cols.start], F32, name="acc")
                 nc.tensor.matmul_mx(
                     out=acc[:],
-                    lhsT=codes[:].bitcast(E4M3X4),
-                    lhsT_scale=plane[:],
+                    lhsT=pa_codes[:].bitcast(E4M3X4),
+                    lhsT_scale=pa_plane[:],
                     rhs=pb_codes[:, cols].bitcast(E4M3X4),
                     rhs_scale=pb_plane[:, cols],
                     start=True,
                     stop=True,
                 )
-                if m >= 2 and h == 1:
-                    nc.vector.tensor_copy(out=res[:, cols], in_=acc[:])
+                if m >= DIRECT and h == 1:
+                    nc.vector.tensor_copy(out=result[:, cols], in_=acc[:])
                 else:
-                    nc.scalar.copy(out=res[:, cols], in_=acc[:])
-            if m in (0, 3):
-                nc.sync.dma_start(out=out[rows, :HALF], in_=res[:, :HALF])
-                nc.sync.dma_start(out=out[rows, HALF:], in_=res[:, HALF:])
-            else:
-                nc.sync.dma_start(out=out[rows, :], in_=res[:])
+                    nc.scalar.copy(out=result[:, cols], in_=acc[:])
+            for h in range(len(store_edges) - 1):
+                cols = slice(store_edges[h], store_edges[h + 1])
+                nc.sync.dma_start(out=out[m * P : (m + 1) * P, cols], in_=result[:, cols])

from contextlib import ExitStack

import concourse.mybir as mybir

K, T, J, R, C, D = 512, 2048, 256, 512, 512, 512
FLOPS = 2 * K * R * J * 2 + 2 * R * C * D

F32 = mybir.dt.float32
BF16 = mybir.dt.bfloat16
I32 = mybir.dt.int32
U32 = mybir.dt.uint32
U16 = mybir.dt.uint16
U8 = mybir.dt.uint8
E4M3X4 = mybir.dt.float8_e4m3fn_x4
E5M2X4 = mybir.dt.float8_e5m2_x4
E2M1X4 = mybir.dt.float4_e2m1fn_x4
COPY = mybir.ActivationFunctionType.Copy

P = 128
PACK = 4
BLOCKS = R // 32
QUADS = 4
LIVE = 4
BANKS = 8
C_TILES = C // P
HALF, QUARTER = D // 2, D // 4
A_BOARDS = 2
DIRECT = 2
RUN = 4


def tile_list_boardsproduct_kernel(tc, xt_words, xt_scales, w_words, w_scales, w2_words, w2_scales, offs, offs2, offs3, offs4, out):
    nc = tc.nc
    with ExitStack() as ctx:
        keep = ctx.enter_context(tc.tile_pool(name="keep", bufs=1))
        psum = ctx.enter_context(tc.psum_pool(name="psum", bufs=BANKS))

        def sb(name, shape, dtype, tag=None):
            return keep.tile(shape, dtype, name=name, tag=tag or name, align_bytes=64)

        list1, list2, list3, list4 = [sb(f"list{i}", [P, J // 16], U16) for i in range(4)]
        x_words = sb("x_words", [P, T], U32)
        x_plane = sb("x_plane", [P, T], U8)
        w_raw = sb("w_raw", [P, R // 2], U32)
        w2_raw = sb("w2_raw", [P, R], U32)
        w_rows = sb("w_rows", [LIVE, QUADS, R // 4], I32)
        w2_rows = sb("w2_rows", [LIVE, QUADS, R // 4], I32)
        w_dealt = sb("w_dealt", [P, PACK, P // 2], U32)
        w2_dealt_first = sb("w2_dealt_first", [P, 1, P], U32)
        w2_dealt_rest = sb("w2_dealt_rest", [P, PACK - 1, P], U32)
        w_plane = sb("w_plane", [P, R], U8)
        w2_plane = sb("w2_plane", [P, R], U8)
        a_boards = [sb(f"a_board{i}", [P, C], F32) for i in range(A_BOARDS)]
        b_boards = [sb(f"b_board{t}", [P, D], F32) for t in range(PACK)]

        nc.vector.memset(x_plane[:].bitcast(I32), 0)
        nc.vector.memset(w2_plane[:].bitcast(I32), 0)
        nc.vector.memset(w_plane[:].bitcast(I32), 0)
        for board in b_boards:
            nc.vector.memset(board[:], 0.0)
        for board in a_boards:
            nc.gpsimd.memset(board[:], 0.0)

        def load_rows(queue, rows, scales):
            queue.dma_start(out=rows[:], in_=scales[0].bitcast(I32).rearrange("(g i) c -> i g c", i=LIVE))

        load_rows(nc.scalar, w2_rows, w2_scales)
        nc.sync.dma_start(list2[:], offs2)
        nc.sync.dma_start(out=x_words[:].bitcast(I32), in_=xt_words[0].rearrange("p n t -> p (n t)").bitcast(I32))
        for i in range(LIVE):
            nc.sync.dma_start(out=x_plane[i:P:32, :].bitcast(I32), in_=xt_scales[0, i : QUADS * LIVE : LIVE, :].bitcast(I32))
        nc.sync.dma_start(out=w2_raw[:].bitcast(I32), in_=w2_words[0].rearrange("p n t -> p (n t)").bitcast(I32))
        nc.sync.dma_start(list4[:], offs4)
        nc.sync.dma_start(list1[:], offs)
        load_rows(nc.sync, w_rows, w_scales)
        nc.sync.dma_start(out=w_raw[:].bitcast(I32), in_=w_words[0].bitcast(I32))
        nc.sync.dma_start(list3[:], offs3)

        def by_slice(columns):
            return columns.rearrange("p (n t u) -> p t n u", t=PACK, n=BLOCKS)

        def deal_plane(plane, rows):
            for g in range(QUADS):
                nc.vector.tensor_copy(
                    out=plane[32 * g : 32 * g + LIVE, :].bitcast(I32).rearrange("p (t n u) -> p t n u", t=PACK, n=BLOCKS),
                    in_=by_slice(rows[:, g, :]),
                )

        def deal_words(copy, dealt, raw_by_slice):
            copy(out=dealt[:].rearrange("p t (n u) -> p t n u", n=BLOCKS), in_=raw_by_slice)

        def gather(name, offsets):
            words = sb(name + "_words", [P, J], U32)
            plane = sb(name + "_plane", [P, J], U8)
            nc.vector.tensor_copy(words[:], x_words[:].indirect(offsets[:]))
            nc.vector.tensor_copy(plane[:], x_plane[:].indirect(offsets[:]))
            return words, plane

        def first_product(name, codes, plane, picked, fetch, width):
            picked_words, picked_plane = picked
            values = sb(name, [P, J], F32)
            for j0 in range(0, J, width):
                slots = slice(j0, j0 + width)
                acc = psum.tile([P, width], F32, name="acc")
                nc.tensor.matmul_mx(
                    out=acc[:],
                    lhsT=codes,
                    lhsT_scale=plane,
                    rhs=picked_words[:, slots].bitcast(E4M3X4),
                    rhs_scale=picked_plane[:, slots],
                    start=True,
                    stop=True,
                )
                fetch(out=values[:, slots], in_=acc[:])
            return values

        deal_plane(w2_plane, w2_rows)
        picked_b = gather("xb", list2)
        deal_words(nc.scalar.copy, w2_dealt_first, by_slice(w2_raw[:])[:, :1])
        deal_words(nc.scalar.copy, w2_dealt_rest, by_slice(w2_raw[:])[:, 1:])
        b = [first_product("b0", w2_dealt_first[:, 0, :].bitcast(E5M2X4), w2_plane[:, :P], picked_b, nc.scalar.copy, J // 2)]
        for t in range(1, PACK):
            codes = w2_dealt_rest[:, t - 1, :].bitcast(E5M2X4)
            b.append(first_product(f"b{t}", codes, w2_plane[:, t * P : (t + 1) * P], picked_b, nc.vector.tensor_copy, J))

        picked_a = gather("xa", list1)
        deal_plane(w_plane, w_rows)
        deal_words(nc.vector.tensor_copy, w_dealt, by_slice(w_raw[:]))
        a = [
            first_product(f"a{t}", w_dealt[:, t, :].bitcast(E2M1X4), w_plane[:, t * P : (t + 1) * P], picked_a, nc.vector.tensor_copy, J)
            for t in range(PACK)
        ]

        pb_woven = sb("pb_woven", [P, D, PACK], BF16, tag="w_raw")
        for t in range(PACK):
            nc.scalar.activation(out=b_boards[t][:].indirect(list4[:]), in_=b[t][:], func=COPY)
            nc.vector.tensor_copy(out=pb_woven[:, :, t], in_=b_boards[t][:])
        pb_codes = sb("pb_codes", [P, D], U32)
        pb_plane = sb("pb_plane", [P, D], U8)
        nc.vector.quantize_mx(out=pb_codes[:].bitcast(E4M3X4), scales=pb_plane[:], in_=pb_woven[:].rearrange("p d t -> p (d t)"))

        pa_woven = [sb(f"pa_woven{m}", [P, P, PACK], BF16) for m in range(DIRECT)]
        pa_planar = sb("pa_planar", [P, PACK, C - DIRECT * P], BF16)

        def weave_direct(t, m):
            nc.vector.tensor_copy(out=pa_woven[m][:, :, t], in_=a_boards[t % A_BOARDS][:, m * P : (m + 1) * P])

        for t in range(PACK):
            board = a_boards[t % A_BOARDS]
            nc.scalar.activation(out=board[:].indirect(list3[:]), in_=a[t][:], func=COPY)
            if t < PACK - 1:
                for m in range(DIRECT):
                    weave_direct(t, m)
                nc.vector.tensor_copy(out=pa_planar[:, t, :], in_=board[:, DIRECT * P :])
            else:
                nc.scalar.copy(out=pa_planar[:, t, :], in_=board[:, DIRECT * P :])

        for m in range(C_TILES):
            woven = pa_woven[m % DIRECT]
            if m < DIRECT:
                weave_direct(PACK - 1, m)
            else:
                nc.vector.tensor_copy(
                    out=woven[:].rearrange("p (c i) t -> p c t i", i=RUN),
                    in_=pa_planar[:, :, (m - DIRECT) * P : (m - DIRECT + 1) * P].rearrange("p t (c i) -> p c t i", i=RUN),
                )
            pa_codes = sb(f"pa_codes{m}", [P, P], U32)
            pa_plane = sb(f"pa_plane{m}", [P, P], U8)
            nc.vector.quantize_mx(out=pa_codes[:].bitcast(E4M3X4), scales=pa_plane[:], in_=woven[:].rearrange("p c t -> p (c t)"))

            store_edges = (0, QUARTER, HALF, D) if m == 0 else (0, HALF, D)
            sum_edges = (0, HALF, HALF + QUARTER, D) if m == C_TILES - 1 else store_edges
            result = sb(f"result{m}", [P, D], F32)
            for h in range(len(sum_edges) - 1):
                cols = slice(sum_edges[h], sum_edges[h + 1])
                acc = psum.tile([P, cols.stop - cols.start], F32, name="acc")
                nc.tensor.matmul_mx(
                    out=acc[:],
                    lhsT=pa_codes[:].bitcast(E4M3X4),
                    lhsT_scale=pa_plane[:],
                    rhs=pb_codes[:, cols].bitcast(E4M3X4),
                    rhs_scale=pb_plane[:, cols],
                    start=True,
                    stop=True,
                )
                if m >= DIRECT and h == 1:
                    nc.vector.tensor_copy(out=result[:, cols], in_=acc[:])
                else:
                    nc.scalar.copy(out=result[:, cols], in_=acc[:])
            for h in range(len(store_edges) - 1):
                cols = slice(store_edges[h], store_edges[h + 1])
                nc.sync.dma_start(out=out[m * P : (m + 1) * P, cols], in_=result[:, cols])
